import numpy as np
import ml_dtypes


def mxq(x, axis, fmt="e4m3"):
    dtype, down = {"e4m3": (ml_dtypes.float8_e4m3fn, 7), "e5m2": (ml_dtypes.float8_e5m2, 14)}[fmt]
    v = np.moveaxis(np.asarray(x, np.float32).astype(ml_dtypes.bfloat16).astype(np.float64), axis, -1)
    blocks = v.reshape(v.shape[:-1] + (-1, 32))
    amax = np.abs(blocks).max(-1, keepdims=True)
    byte = np.maximum(np.where(amax > 0, np.frexp(amax)[1] - 1 + 127, 0) - down, 1)
    scale = np.exp2(byte - 127.0)
    codes = (blocks / scale).astype(np.float32).astype(dtype).astype(np.float64)
    return np.moveaxis((codes * scale).reshape(v.shape), -1, axis)


WIDE = False


def mx_kscale(k):
    if not WIDE:
        return np.ones(k)
    levels = np.array([10, -10, 5, -5, 0])
    if k % 512:
        return np.exp2(np.random.permutation(np.resize(levels, k // 32))).repeat(32)
    a = np.empty((k // 512, 16))
    for p in range(k // 512):
        a[p, :8] = np.random.permutation(np.resize(levels, 8))
        for g in range(8):
            far = levels[np.abs(levels - a[p, g]) >= 10]
            a[p, g + 8] = far[np.random.randint(len(far))]
    return np.exp2(a.ravel()).repeat(32)


def f64(x):
    return np.asarray(x).astype(np.float64)


def striped(idx):
    return np.tile(idx.reshape(-1, 16).T, (8, 1)).astype(np.uint16)


def unstriped(offs):
    return offs[:16].T.reshape(-1).astype(np.int64)


def striped8(idx):
    return np.concatenate([x.reshape(-1, 16).T for x in idx]).astype(np.uint16)


def runs(offs, k):
    lists = np.stack([offs[16 * r : 16 * r + 16].T.reshape(-1) for r in range(8)]).astype(np.int64)
    return lists[np.arange(k) % 512 // 64]


def pack_weight(w):
    k, n = w.shape
    w = f64(np.asarray(w, np.float32).astype(ml_dtypes.bfloat16)).reshape(k // 32, 32, n)
    amax = np.abs(w).max(1)
    byte = np.clip(np.where(amax > 0, np.frexp(amax)[1] - 1 + 127 - 7, 1), 1, 254)
    scaled = (w * np.exp2(127.0 - byte)[:, None, :]).reshape(k, n).astype(np.float32)
    words = np.ascontiguousarray(scaled.reshape(k // 512, 128, 4, n).transpose(0, 1, 3, 2)).astype(ml_dtypes.float8_e4m3fn).view(np.uint8)
    return words, np.ascontiguousarray(byte.astype(np.uint8).reshape(k // 512, 16, n))


def unpack_weight(words, scales):
    g, p, n, _ = words.shape
    vals = np.ascontiguousarray(words).view(ml_dtypes.float8_e4m3fn).astype(np.float64) * np.repeat(np.exp2(scales.astype(np.float64) - 127.0), 8, axis=1)[..., None]
    return vals.transpose(0, 1, 3, 2).reshape(g * 512, n)


K, T, S, H, C = 512, 2048, 512, 512, 512


def setup_inputs():
    n = np.random.standard_normal
    s = mx_kscale(K)[:, None]
    packed_xT = pack_weight(n((K, T)) * s)
    return {
        "x_words": packed_xT[0],
        "x_scales": packed_xT[1],
        "w1": (n((K, H)) / np.sqrt(K) / s).astype(np.float32),
        "gs": (np.random.uniform(0.5, 1.5, (K, 1)) / s).astype(np.float32),
        "offs": striped(np.random.permutation(T)[:S]),
        "lf": striped8(np.stack([np.random.permutation(S) for _ in range(8)])),
        "rt": striped8(np.stack([np.random.permutation(S) for _ in range(8)])),
        "cand": striped(np.random.permutation(T)[:C]),
    }


def reference(x_words, x_scales, w1, gs, offs, lf, rt, cand):
    x_cand = unpack_weight(x_words, x_scales)[:, unstriped(cand)]
    xq = unpack_weight(x_words, x_scales)[:, unstriped(offs)]
    y = mxq(f64(w1), 0, "e4m3").T @ xq
    z = f64(gs) * (0.5 * ((y) ** 2 - ((y[np.arange(H)[:, None], runs(lf, H)]) * (y[np.arange(H)[:, None], runs(rt, H)]))))
    return 0.0625 * ((x_cand.T @ mxq(z, 0, "e4m3")))

@@ -1,0 +1,174 @@
+from contextlib import ExitStack
+
+import concourse.mybir as mybir
+
+K, T, S, H, C = 512, 2048, 512, 512, 512
+FLOPS = 2 * K * H * S + 2 * K * C * S
+
+F32 = mybir.dt.float32
+BF16 = mybir.dt.bfloat16
+I32 = mybir.dt.int32
+U32 = mybir.dt.uint32
+U16 = mybir.dt.uint16
+U8 = mybir.dt.uint8
+FP8X4 = mybir.dt.float8_e4m3fn_x4
+MULT = mybir.AluOpType.mult
+SUBTRACT = mybir.AluOpType.subtract
+COPY = mybir.ActivationFunctionType.Copy
+SQUARE = mybir.ActivationFunctionType.Square
+
+P = 128
+PACK = 4
+STRIPE = 16
+WIDE = 384
+W_CHUNKS = 2
+
+
+def entries(offsets, cols):
+    return offsets[:, cols.start // STRIPE : cols.stop // STRIPE]
+
+
+def tile_picked_teager8_none_p_kernel(tc, x_words, x_scales, w1, gs, offs, lf, rt, cand, out):
+    nc = tc.nc
+    with ExitStack() as ctx:
+        held = ctx.enter_context(tc.tile_pool(name="held", bufs=1))
+        ring = ctx.enter_context(tc.tile_pool(name="ring", bufs=2))
+        psum = ctx.enter_context(tc.psum_pool(name="psum", bufs=1))
+
+        offs_sb = held.tile([P, S // STRIPE], U16, name="offs_sb")
+        cand_sb = held.tile([P, C // STRIPE], U16, name="cand_sb")
+        lf_sb = held.tile([P, S // STRIPE], U16, name="lf_sb")
+        rt_sb = held.tile([P, S // STRIPE], U16, name="rt_sb")
+        table_words = held.tile([P, T], U32, name="table_words", align_bytes=64)
+        table_scales = held.tile([P, T], U8, name="table_scales", align_bytes=64)
+        gain = held.tile([P, PACK], F32, name="gain")
+        half_gain = held.tile([P, PACK], F32, name="half_gain")
+        w_width = H // W_CHUNKS
+        w_raw = [held.tile([P, PACK, w_width], F32, name=f"w_raw{c}") for c in range(W_CHUNKS)]
+
+        nc.sync.dma_start(offs_sb[:], offs)
+        for q in range(4):
+            rows = x_scales[0, 4 * q : 4 * q + 4, :].bitcast(I32)
+            nc.scalar.dma_start(table_scales[32 * q : 32 * q + 32, :].bitcast(I32), rows.partition_broadcast(8))
+        nc.sync.dma_start(cand_sb[:], cand)
+        w_rows = w1.rearrange("(p j) h -> p j h", j=PACK)
+        for c in range(W_CHUNKS):
+            nc.sync.dma_start(w_raw[c][:], w_rows[:, :, c * w_width : (c + 1) * w_width])
+        nc.sync.dma_start(table_words[:].bitcast(I32), x_words[0].rearrange("p n t -> p (n t)").bitcast(I32))
+        nc.sync.dma_start(gain[:], gs.rearrange("(p t) o -> p (t o)", t=PACK))
+        nc.sync.dma_start(lf_sb[:], lf)
+        nc.sync.dma_start(rt_sb[:], rt)
+
+        q_scales = held.tile([P, S], U8, name="q_scales", align_bytes=64)
+        c_scales = held.tile([P, C], U8, name="c_scales", align_bytes=64)
+        nc.vector.tensor_copy(q_scales[:], table_scales[:].indirect(offs_sb[:]))
+        nc.vector.tensor_copy(c_scales[:], table_scales[:].indirect(cand_sb[:]))
+
+        w_grouped = held.tile([P, H * PACK], BF16, name="w_grouped", align_bytes=64)
+        w_dealt = w_grouped[:].rearrange("p (t m j) -> p m t j", t=PACK, j=PACK)
+        m_width = w_width // PACK
+        for c in range(W_CHUNKS):
+            nc.scalar.activation(w_dealt[:, c * m_width : (c + 1) * m_width], w_raw[c][:].rearrange("p j (m t) -> p m t j", t=PACK), COPY)
+        nc.scalar.activation(half_gain[:], gain[:], COPY, scale=0.5)
+        w_words = held.tile([P, H], U32, name="w_words", align_bytes=64)
+        w_scales = held.tile([P, H], U8, name="w_scales", align_bytes=64)
+        for h in range(2):
+            cols = slice(h * 256, (h + 1) * 256)
+            nc.vector.quantize_mx(w_words[:, cols].bitcast(FP8X4), w_scales[:, cols], w_grouped[:, cols.start * PACK : cols.stop * PACK])
+
+        halves = [slice(0, S // 2), slice(S // 2, S)]
+        q_words = [held.tile([P, S // 2], U32, name=f"q_words{h}", align_bytes=64) for h in range(2)]
+        for h, cols in enumerate(halves):
+            nc.vector.tensor_copy(q_words[h][:], table_words[:].indirect(entries(offs_sb, cols)))
+        c_words = held.tile([P, C], U32, name="c_words", align_bytes=64)
+        nc.vector.tensor_copy(c_words[:], table_words[:].indirect(cand_sb[:]))
+
+        y_bank = [psum.tile([P, S], F32, name=f"y_bank{t}") for t in range(PACK)]
+        for h, cols in enumerate(halves):
+            for t in range(PACK):
+                rows = slice(t * P, (t + 1) * P)
+                nc.tensor.matmul_mx(y_bank[t][:, cols], lhsT=w_words[:, rows].bitcast(FP8X4), lhsT_scale=w_scales[:, rows],
+                                    rhs=q_words[h][:].bitcast(FP8X4), rhs_scale=q_scales[:, cols], start=True, stop=True)
+
+        y = [held.tile([P, S], F32, name=f"y{t}") for t in range(PACK)]
+        gy = [held.tile([P, S], F32, name=f"gy{t}") for t in range(PACK)]
+        gyy = held.tile([P, PACK, S], F32, name="gyy")
+
+        def plain(t):
+            nc.scalar.copy(y[t][:], y_bank[t][:])
+
+        def weighted(t):
+            nc.scalar.activation(gy[t][:], y_bank[t][:], COPY, scale=half_gain[:, t : t + 1])
+
+        def squared(t):
+            yy = ring.tile([P, S], F32, name="yy")
+            nc.scalar.activation(yy[:], y_bank[t][:], SQUARE)
+            nc.scalar.activation(gyy[:, t, :], yy[:], COPY, scale=half_gain[:, t : t + 1])
+
+        plain(0)
+        for t in range(PACK):
+            if t + 1 < PACK:
+                plain(t + 1)
+            weighted(t)
+            if t >= 1:
+                squared(t - 1)
+        squared(PACK - 1)
+
+        z_words = held.tile([P, S], U32, name="z_words", align_bytes=64)
+        z_scales = held.tile([P, S], U8, name="z_scales", align_bytes=64)
+        z_grouped = held.tile([P, S * PACK], BF16, name="z_grouped", align_bytes=64)
+        out_rows = out.rearrange("(i p) j -> p i j", p=P)
+
+        def fetch_left(t, cols):
+            left = ring.tile([P, cols.stop - cols.start], F32, name="left")
+            nc.vector.tensor_copy(left[:], y[t][:].indirect(entries(lf_sb, cols)))
+            return left
+
+        def times_right(prod, t, cols, left):
+            nc.vector.tensor_tensor(prod[:, t, :], gy[t][:].indirect(entries(rt_sb, cols)), left[:], MULT)
+
+        def subtract(prod, cols):
+            z_cols = z_grouped[:, cols.start * PACK : cols.stop * PACK].rearrange("p (c i t) -> p c t i", i=4, t=PACK)
+            nc.vector.tensor_tensor(z_cols, gyy[:, :, cols].rearrange("p t (c i) -> p c t i", i=4),
+                                    prod[:].rearrange("p t (c i) -> p c t i", i=4), SUBTRACT)
+
+        def score(cols, tags):
+            width = cols.stop - cols.start
+            nc.vector.quantize_mx(z_words[:, cols].bitcast(FP8X4), z_scales[:, cols], z_grouped[:, cols.start * PACK : cols.stop * PACK])
+            per_bank = C // P // len(tags)
+            banks = [psum.tile([P, per_bank, width], F32, name=tag) for tag in tags]
+            for i in range(C // P):
+                rows = slice(i * P, (i + 1) * P)
+                nc.tensor.matmul_mx(banks[i // per_bank][:, i % per_bank, :], lhsT=c_words[:, rows].bitcast(FP8X4), lhsT_scale=c_scales[:, rows],
+                                    rhs=z_words[:, cols].bitcast(FP8X4), rhs_scale=z_scales[:, cols], start=True, stop=True)
+            return banks
+
+        def store(cols, banks, on_vector):
+            per_bank = C // P // len(banks)
+            for b, bank in enumerate(banks):
+                staged = held.tile([P, per_bank, cols.stop - cols.start], F32, name=f"staged{cols.start}_{b}")
+                rows = out_rows[:, b * per_bank : (b + 1) * per_bank, cols]
+                if b in on_vector:
+                    nc.vector.tensor_scalar_mul(staged[:], bank[:], 0.0625)
+                    nc.sync.dma_start(rows, staged[:])
+                else:
+                    nc.scalar.activation(staged[:], bank[:], COPY, scale=0.0625)
+                    (nc.scalar if on_vector else nc.sync).dma_start(rows, staged[:])
+
+        wide, last = slice(0, WIDE), slice(WIDE, S)
+        steps = [(cols, t) for cols in (wide, last) for t in range(PACK)]
+        prod = held.tile([P, PACK, WIDE], F32, name="prod")
+        left = fetch_left(0, wide)
+        for n, (cols, t) in enumerate(steps):
+            nxt = fetch_left(steps[n + 1][1], steps[n + 1][0]) if n + 1 < len(steps) else None
+            if n == PACK:
+                subtract(prod, wide)
+                prod = held.tile([P, PACK, S - WIDE], F32, name="prod")
+            times_right(prod, t, cols, left)
+            left = nxt
+            if n == PACK:
+                store(slice(0, 256), score(slice(0, 256), ["score_a", "score_b"]), [])
+            if n == PACK + 1:
+                store(slice(256, WIDE), score(slice(256, WIDE), ["score_c"]), [])
+        subtract(prod, last)
+        store(last, score(last, ["score_d", "y_bank0"]), [1])

@@ -46,14 +46,14 @@ def tile_picked_teager8_none_p_kernel(tc, x_words, x_scales, w1, gs, offs, lf, r
         w_width = H // W_CHUNKS
         w_raw = [held.tile([P, PACK, w_width], F32, name=f"w_raw{c}") for c in range(W_CHUNKS)]
 
+        nc.vector.memset(table_scales[:].bitcast(I32), 0)
         nc.sync.dma_start(offs_sb[:], offs)
-        for q in range(4):
-            rows = x_scales[0, 4 * q : 4 * q + 4, :].bitcast(I32)
-            nc.scalar.dma_start(table_scales[32 * q : 32 * q + 32, :].bitcast(I32), rows.partition_broadcast(8))
         nc.sync.dma_start(cand_sb[:], cand)
         w_rows = w1.rearrange("(p j) h -> p j h", j=PACK)
-        for c in range(W_CHUNKS):
-            nc.sync.dma_start(w_raw[c][:], w_rows[:, :, c * w_width : (c + 1) * w_width])
+        nc.sync.dma_start(w_raw[0][:], w_rows[:, :, :w_width])
+        for q in range(4):
+            nc.sync.dma_start(table_scales[32 * q : 32 * q + 4, :].bitcast(I32), x_scales[0, 4 * q : 4 * q + 4, :].bitcast(I32))
+        nc.sync.dma_start(w_raw[1][:], w_rows[:, :, w_width:])
         nc.sync.dma_start(table_words[:].bitcast(I32), x_words[0].rearrange("p n t -> p (n t)").bitcast(I32))
         nc.sync.dma_start(gain[:], gs.rearrange("(p t) o -> p (t o)", t=PACK))
         nc.sync.dma_start(lf_sb[:], lf)
@@ -92,6 +92,7 @@ def tile_picked_teager8_none_p_kernel(tc, x_words, x_scales, w1, gs, offs, lf, r
 
         y = [held.tile([P, S], F32, name=f"y{t}") for t in range(PACK)]
         gy = [held.tile([P, S], F32, name=f"gy{t}") for t in range(PACK)]
+        yy = [held.tile([P, S], F32, name=f"yy{t}") for t in range(PACK)]
         gyy = held.tile([P, PACK, S], F32, name="gyy")
 
         def plain(t):
@@ -101,18 +102,24 @@ def tile_picked_teager8_none_p_kernel(tc, x_words, x_scales, w1, gs, offs, lf, r
             nc.scalar.activation(gy[t][:], y_bank[t][:], COPY, scale=half_gain[:, t : t + 1])
 
         def squared(t):
-            yy = ring.tile([P, S], F32, name="yy")
-            nc.scalar.activation(yy[:], y_bank[t][:], SQUARE)
-            nc.scalar.activation(gyy[:, t, :], yy[:], COPY, scale=half_gain[:, t : t + 1])
+            nc.scalar.activation(yy[t][:], y_bank[t][:], SQUARE)
 
+        def weighted_square(t, cols):
+            nc.scalar.activation(gyy[:, t, cols], yy[t][:, cols], COPY, scale=half_gain[:, t : t + 1])
+
+        wide, last = slice(0, WIDE), slice(WIDE, S)
         plain(0)
+        plain(1)
+        weighted(0)
         for t in range(PACK):
+            if t + 2 < PACK:
+                plain(t + 2)
+            squared(t)
             if t + 1 < PACK:
-                plain(t + 1)
-            weighted(t)
-            if t >= 1:
-                squared(t - 1)
-        squared(PACK - 1)
+                weighted(t + 1)
+            weighted_square(t, wide)
+        for t in range(PACK):
+            weighted_square(t, last)
 
         z_words = held.tile([P, S], U32, name="z_words", align_bytes=64)
         z_scales = held.tile([P, S], U8, name="z_scales", align_bytes=64)
@@ -125,12 +132,12 @@ def tile_picked_teager8_none_p_kernel(tc, x_words, x_scales, w1, gs, offs, lf, r
             return left
 
         def times_right(prod, t, cols, left):
-            nc.vector.tensor_tensor(prod[:, t, :], gy[t][:].indirect(entries(rt_sb, cols)), left[:], MULT)
+            nc.vector.tensor_tensor(prod[:, t, : cols.stop - cols.start], gy[t][:].indirect(entries(rt_sb, cols)), left[:], MULT)
 
-        def subtract(prod, cols):
+        def subtract(prod, cols, at):
             z_cols = z_grouped[:, cols.start * PACK : cols.stop * PACK].rearrange("p (c i t) -> p c t i", i=4, t=PACK)
             nc.vector.tensor_tensor(z_cols, gyy[:, :, cols].rearrange("p t (c i) -> p c t i", i=4),
-                                    prod[:].rearrange("p t (c i) -> p c t i", i=4), SUBTRACT)
+                                    prod[:, :, at : at + cols.stop - cols.start].rearrange("p t (c i) -> p c t i", i=4), SUBTRACT)
 
         def score(cols, tags):
             width = cols.stop - cols.start
@@ -155,20 +162,19 @@ def tile_picked_teager8_none_p_kernel(tc, x_words, x_scales, w1, gs, offs, lf, r
                     nc.scalar.activation(staged[:], bank[:], COPY, scale=0.0625)
                     (nc.scalar if on_vector else nc.sync).dma_start(rows, staged[:])
 
-        wide, last = slice(0, WIDE), slice(WIDE, S)
+        first, second = slice(0, 256), slice(256, WIDE)
         steps = [(cols, t) for cols in (wide, last) for t in range(PACK)]
         prod = held.tile([P, PACK, WIDE], F32, name="prod")
         left = fetch_left(0, wide)
         for n, (cols, t) in enumerate(steps):
             nxt = fetch_left(steps[n + 1][1], steps[n + 1][0]) if n + 1 < len(steps) else None
             if n == PACK:
-                subtract(prod, wide)
-                prod = held.tile([P, PACK, S - WIDE], F32, name="prod")
+                subtract(prod, first, 0)
+                subtract(prod, second, 256)
             times_right(prod, t, cols, left)
             left = nxt
             if n == PACK:
-                store(slice(0, 256), score(slice(0, 256), ["score_a", "score_b"]), [])
-            if n == PACK + 1:
-                store(slice(256, WIDE), score(slice(256, WIDE), ["score_c"]), [])
-        subtract(prod, last)
+                store(first, score(first, ["score_a", "score_b"]), [])
+        store(second, score(second, ["score_c"]), [])
+        subtract(prod, last, 0)
         store(last, score(last, ["score_d", "y_bank0"]), [1])

@@ -32,7 +32,6 @@ def tile_picked_teager8_none_p_kernel(tc, x_words, x_scales, w1, gs, offs, lf, r
     nc = tc.nc
     with ExitStack() as ctx:
         held = ctx.enter_context(tc.tile_pool(name="held", bufs=1))
-        ring = ctx.enter_context(tc.tile_pool(name="ring", bufs=2))
         psum = ctx.enter_context(tc.psum_pool(name="psum", bufs=1))
 
         offs_sb = held.tile([P, S // STRIPE], U16, name="offs_sb")
@@ -104,8 +103,8 @@ def tile_picked_teager8_none_p_kernel(tc, x_words, x_scales, w1, gs, offs, lf, r
         def squared(t):
             nc.scalar.activation(yy[t][:], y_bank[t][:], SQUARE)
 
-        def weighted_square(t, cols):
-            nc.scalar.activation(gyy[:, t, cols], yy[t][:, cols], COPY, scale=half_gain[:, t : t + 1])
+        def weighted_square(t):
+            nc.scalar.activation(gyy[:, t, :], yy[t][:], COPY, scale=half_gain[:, t : t + 1])
 
         wide, last = slice(0, WIDE), slice(WIDE, S)
         plain(0)
@@ -117,9 +116,7 @@ def tile_picked_teager8_none_p_kernel(tc, x_words, x_scales, w1, gs, offs, lf, r
             squared(t)
             if t + 1 < PACK:
                 weighted(t + 1)
-            weighted_square(t, wide)
-        for t in range(PACK):
-            weighted_square(t, last)
+            weighted_square(t)
 
         z_words = held.tile([P, S], U32, name="z_words", align_bytes=64)
         z_scales = held.tile([P, S], U8, name="z_scales", align_bytes=64)
@@ -127,7 +124,8 @@ def tile_picked_teager8_none_p_kernel(tc, x_words, x_scales, w1, gs, offs, lf, r
         out_rows = out.rearrange("(i p) j -> p i j", p=P)
 
         def fetch_left(t, cols):
-            left = ring.tile([P, cols.stop - cols.start], F32, name="left")
+            name = "yy2" if (t, cols) == (PACK - 1, last) else f"left{t}_{cols.start}"
+            left = held.tile([P, cols.stop - cols.start], F32, name=name)
             nc.vector.tensor_copy(left[:], y[t][:].indirect(entries(lf_sb, cols)))
             return left
 
@@ -135,9 +133,9 @@ def tile_picked_teager8_none_p_kernel(tc, x_words, x_scales, w1, gs, offs, lf, r
             nc.vector.tensor_tensor(prod[:, t, : cols.stop - cols.start], gy[t][:].indirect(entries(rt_sb, cols)), left[:], MULT)
 
         def subtract(prod, cols, at):
-            z_cols = z_grouped[:, cols.start * PACK : cols.stop * PACK].rearrange("p (c i t) -> p c t i", i=4, t=PACK)
-            nc.vector.tensor_tensor(z_cols, gyy[:, :, cols].rearrange("p t (c i) -> p c t i", i=4),
-                                    prod[:, :, at : at + cols.stop - cols.start].rearrange("p t (c i) -> p c t i", i=4), SUBTRACT)
+            z_cols = z_grouped[:, cols.start * PACK : cols.stop * PACK].rearrange("p (c i t) -> p c t i", i=2, t=PACK)
+            nc.vector.tensor_tensor(z_cols, gyy[:, :, cols].rearrange("p t (c i) -> p c t i", i=2),
+                                    prod[:, :, at : at + cols.stop - cols.start].rearrange("p t (c i) -> p c t i", i=2), SUBTRACT)
 
         def score(cols, tags):
             width = cols.stop - cols.start
@@ -163,17 +161,21 @@ def tile_picked_teager8_none_p_kernel(tc, x_words, x_scales, w1, gs, offs, lf, r
                     (nc.scalar if on_vector else nc.sync).dma_start(rows, staged[:])
 
         first, second = slice(0, 256), slice(256, WIDE)
-        steps = [(cols, t) for cols in (wide, last) for t in range(PACK)]
         prod = held.tile([P, PACK, WIDE], F32, name="prod")
-        left = fetch_left(0, wide)
-        for n, (cols, t) in enumerate(steps):
-            nxt = fetch_left(steps[n + 1][1], steps[n + 1][0]) if n + 1 < len(steps) else None
-            if n == PACK:
-                subtract(prod, first, 0)
-                subtract(prod, second, 256)
-            times_right(prod, t, cols, left)
-            left = nxt
-            if n == PACK:
+        left_wide, left_last = [], []
+        for t in range(PACK):
+            left_wide.append(fetch_left(t, wide))
+            if t < PACK - 1:
+                left_last.append(fetch_left(t, last))
+            if t >= 1:
+                times_right(prod, t - 1, wide, left_wide[t - 1])
+        times_right(prod, PACK - 1, wide, left_wide[PACK - 1])
+        left_last.append(fetch_left(PACK - 1, last))
+        subtract(prod, first, 0)
+        subtract(prod, second, 256)
+        for t in range(PACK):
+            times_right(prod, t, last, left_last[t])
+            if t == 0:
                 store(first, score(first, ["score_a", "score_b"]), [])
         store(second, score(second, ["score_c"]), [])
         subtract(prod, last, 0)

@@ -50,8 +50,8 @@ def tile_picked_teager8_none_p_kernel(tc, x_words, x_scales, w1, gs, offs, lf, r
         nc.sync.dma_start(cand_sb[:], cand)
         w_rows = w1.rearrange("(p j) h -> p j h", j=PACK)
         nc.sync.dma_start(w_raw[0][:], w_rows[:, :, :w_width])
-        for q in range(4):
-            nc.sync.dma_start(table_scales[32 * q : 32 * q + 4, :].bitcast(I32), x_scales[0, 4 * q : 4 * q + 4, :].bitcast(I32))
+        for r in range(4):
+            nc.sync.dma_start(table_scales[r:P:32, :].bitcast(I32), x_scales[0, r:16:4, :].bitcast(I32))
         nc.sync.dma_start(w_raw[1][:], w_rows[:, :, w_width:])
         nc.sync.dma_start(table_words[:].bitcast(I32), x_words[0].rearrange("p n t -> p (n t)").bitcast(I32))
         nc.sync.dma_start(gain[:], gs.rearrange("(p t) o -> p (t o)", t=PACK))
@@ -83,15 +83,14 @@ def tile_picked_teager8_none_p_kernel(tc, x_words, x_scales, w1, gs, offs, lf, r
         nc.vector.tensor_copy(c_words[:], table_words[:].indirect(cand_sb[:]))
 
         y_bank = [psum.tile([P, S], F32, name=f"y_bank{t}") for t in range(PACK)]
-        for h, cols in enumerate(halves):
-            for t in range(PACK):
-                rows = slice(t * P, (t + 1) * P)
+        for t in range(PACK):
+            rows = slice(t * P, (t + 1) * P)
+            for h, cols in enumerate(halves):
                 nc.tensor.matmul_mx(y_bank[t][:, cols], lhsT=w_words[:, rows].bitcast(FP8X4), lhsT_scale=w_scales[:, rows],
                                     rhs=q_words[h][:].bitcast(FP8X4), rhs_scale=q_scales[:, cols], start=True, stop=True)
 
         y = [held.tile([P, S], F32, name=f"y{t}") for t in range(PACK)]
         gy = [held.tile([P, S], F32, name=f"gy{t}") for t in range(PACK)]
-        yy = [held.tile([P, S], F32, name=f"yy{t}") for t in range(PACK)]
         gyy = held.tile([P, PACK, S], F32, name="gyy")
 
         def plain(t):
@@ -100,23 +99,28 @@ def tile_picked_teager8_none_p_kernel(tc, x_words, x_scales, w1, gs, offs, lf, r
         def weighted(t):
             nc.scalar.activation(gy[t][:], y_bank[t][:], COPY, scale=half_gain[:, t : t + 1])
 
-        def squared(t):
-            nc.scalar.activation(yy[t][:], y_bank[t][:], SQUARE)
+        def squared(t, cols):
+            yy = held.tile([P, cols.stop - cols.start], F32, name=f"yy{t}_{cols.start}")
+            nc.scalar.activation(yy[:], y_bank[t][:, cols], SQUARE)
+            return yy
 
-        def weighted_square(t):
-            nc.scalar.activation(gyy[:, t, :], yy[t][:], COPY, scale=half_gain[:, t : t + 1])
+        def weighted_square(t, cols, yy):
+            nc.scalar.activation(gyy[:, t, cols], yy[:], COPY, scale=half_gain[:, t : t + 1])
 
         wide, last = slice(0, WIDE), slice(WIDE, S)
         plain(0)
-        plain(1)
-        weighted(0)
         for t in range(PACK):
-            if t + 2 < PACK:
-                plain(t + 2)
-            squared(t)
             if t + 1 < PACK:
-                weighted(t + 1)
-            weighted_square(t)
+                plain(t + 1)
+            weighted(t)
+        yy = squared(0, wide)
+        for t in range(PACK):
+            yy_ahead = squared(t + 1, wide) if t + 1 < PACK else None
+            weighted_square(t, wide, yy)
+            yy = yy_ahead
+        yy_last = [squared(t, last) for t in range(PACK)]
+        for t in range(PACK):
+            weighted_square(t, last, yy_last[t])
 
         z_words = held.tile([P, S], U32, name="z_words", align_bytes=64)
         z_scales = held.tile([P, S], U8, name="z_scales", align_bytes=64)
@@ -124,7 +128,7 @@ def tile_picked_teager8_none_p_kernel(tc, x_words, x_scales, w1, gs, offs, lf, r
         out_rows = out.rearrange("(i p) j -> p i j", p=P)
 
         def fetch_left(t, cols):
-            name = "yy2" if (t, cols) == (PACK - 1, last) else f"left{t}_{cols.start}"
+            name = f"left{t}" if cols == wide else ["left_last0", "yy0_0", "yy3_0", f"yy0_{WIDE}"][t]
             left = held.tile([P, cols.stop - cols.start], F32, name=name)
             nc.vector.tensor_copy(left[:], y[t][:].indirect(entries(lf_sb, cols)))
             return left
@@ -162,21 +166,28 @@ def tile_picked_teager8_none_p_kernel(tc, x_words, x_scales, w1, gs, offs, lf, r
 
         first, second = slice(0, 256), slice(256, WIDE)
         prod = held.tile([P, PACK, WIDE], F32, name="prod")
-        left_wide, left_last = [], []
+        left = fetch_left(0, wide)
+        left_last = [fetch_left(0, last)]
         for t in range(PACK):
-            left_wide.append(fetch_left(t, wide))
-            if t < PACK - 1:
-                left_last.append(fetch_left(t, last))
-            if t >= 1:
-                times_right(prod, t - 1, wide, left_wide[t - 1])
-        times_right(prod, PACK - 1, wide, left_wide[PACK - 1])
-        left_last.append(fetch_left(PACK - 1, last))
+            ahead = fetch_left(t + 1, wide) if t + 1 < PACK else None
+            times_right(prod, t, wide, left)
+            left = ahead
+        left_last.append(fetch_left(1, last))
         subtract(prod, first, 0)
+        left_last.append(fetch_left(2, last))
+        store(first, score(first, ["score_a", "score_b"]), [])
         subtract(prod, second, 256)
-        for t in range(PACK):
+        times_right(prod, 0, last, left_last[0])
+        left_last.append(fetch_left(3, last))
+        for t in range(1, PACK):
             times_right(prod, t, last, left_last[t])
-            if t == 0:
-                store(first, score(first, ["score_a", "score_b"]), [])
         store(second, score(second, ["score_c"]), [])
         subtract(prod, last, 0)
-        store(last, score(last, ["score_d", "y_bank0"]), [1])
+        banks = score(last, ["score_d", "y_bank0", "y_bank1", "y_bank2"])
+        by_scalar = held.tile([P, 2, S - WIDE], F32, name="by_scalar")
+        by_vector = held.tile([P, 2, S - WIDE], F32, name="by_vector")
+        for n in range(2):
+            nc.scalar.activation(by_scalar[:, n, :], banks[2 * n][:, 0, :], COPY, scale=0.0625)
+            nc.vector.tensor_scalar_mul(by_vector[:, n, :], banks[2 * n + 1][:, 0, :], 0.0625)
+        nc.scalar.dma_start(out_rows[:, 0::2, last], by_scalar[:])
+        nc.sync.dma_start(out_rows[:, 1::2, last], by_vector[:])

@@ -1,6 +1,7 @@
 from contextlib import ExitStack
 
 import concourse.mybir as mybir
+from concourse.masks import make_identity
 
 K, T, S, H, C = 512, 2048, 512, 512, 512
 FLOPS = 2 * K * H * S + 2 * K * C * S
@@ -13,7 +14,7 @@ U16 = mybir.dt.uint16
 U8 = mybir.dt.uint8
 FP8X4 = mybir.dt.float8_e4m3fn_x4
 MULT = mybir.AluOpType.mult
-SUBTRACT = mybir.AluOpType.subtract
+ADD = mybir.AluOpType.add
 COPY = mybir.ActivationFunctionType.Copy
 SQUARE = mybir.ActivationFunctionType.Square
 
@@ -69,6 +70,10 @@ def tile_picked_teager8_none_p_kernel(tc, x_words, x_scales, w1, gs, offs, lf, r
         for c in range(W_CHUNKS):
             nc.scalar.activation(w_dealt[:, c * m_width : (c + 1) * m_width], w_raw[c][:].rearrange("p j (m t) -> p m t j", t=PACK), COPY)
         nc.scalar.activation(half_gain[:], gain[:], COPY, scale=0.5)
+        minus_half_gain = held.tile([P, PACK], F32, name="minus_half_gain")
+        nc.scalar.activation(minus_half_gain[:], gain[:], COPY, scale=-0.5)
+        identity = held.tile([P, P], F32, name="identity")
+        make_identity(nc, identity[:])
         w_words = held.tile([P, H], U32, name="w_words", align_bytes=64)
         w_scales = held.tile([P, H], U8, name="w_scales", align_bytes=64)
         for h in range(2):
@@ -91,21 +96,21 @@ def tile_picked_teager8_none_p_kernel(tc, x_words, x_scales, w1, gs, offs, lf, r
 
         y = [held.tile([P, S], F32, name=f"y{t}") for t in range(PACK)]
         gy = [held.tile([P, S], F32, name=f"gy{t}") for t in range(PACK)]
-        gyy = held.tile([P, PACK, S], F32, name="gyy")
+        gyy = held.tile([P, PACK, WIDE], F32, name="gyy")
 
         def plain(t):
             nc.scalar.copy(y[t][:], y_bank[t][:])
 
         def weighted(t):
-            nc.scalar.activation(gy[t][:], y_bank[t][:], COPY, scale=half_gain[:, t : t + 1])
+            nc.scalar.activation(gy[t][:], y_bank[t][:], COPY, scale=minus_half_gain[:, t : t + 1])
 
         def squared(t, cols):
             yy = held.tile([P, cols.stop - cols.start], F32, name=f"yy{t}_{cols.start}")
-            nc.scalar.activation(yy[:], y_bank[t][:, cols], SQUARE)
+            nc.scalar.activation(yy[:], y[t][:, cols], SQUARE)
             return yy
 
-        def weighted_square(t, cols, yy):
-            nc.scalar.activation(gyy[:, t, cols], yy[:], COPY, scale=half_gain[:, t : t + 1])
+        def weighted_square(t, into, yy):
+            nc.scalar.activation(into[:, t, :], yy[:], COPY, scale=half_gain[:, t : t + 1])
 
         wide, last = slice(0, WIDE), slice(WIDE, S)
         plain(0)
@@ -116,34 +121,35 @@ def tile_picked_teager8_none_p_kernel(tc, x_words, x_scales, w1, gs, offs, lf, r
         yy = squared(0, wide)
         for t in range(PACK):
             yy_ahead = squared(t + 1, wide) if t + 1 < PACK else None
-            weighted_square(t, wide, yy)
+            weighted_square(t, gyy, yy)
             yy = yy_ahead
         yy_last = [squared(t, last) for t in range(PACK)]
-        for t in range(PACK):
-            weighted_square(t, last, yy_last[t])
 
         z_words = held.tile([P, S], U32, name="z_words", align_bytes=64)
         z_scales = held.tile([P, S], U8, name="z_scales", align_bytes=64)
-        z_grouped = held.tile([P, S * PACK], BF16, name="z_grouped", align_bytes=64)
+        first, second = slice(0, 256), slice(256, WIDE)
+        z_grouped = {cols.start: held.tile([P, (cols.stop - cols.start) * PACK], BF16, name=f"z_grouped{cols.start}", align_bytes=64)
+                     for cols in (first, second, last)}
         out_rows = out.rearrange("(i p) j -> p i j", p=P)
 
-        def fetch_left(t, cols):
-            name = f"left{t}" if cols == wide else ["left_last0", "yy0_0", "yy3_0", f"yy0_{WIDE}"][t]
-            left = held.tile([P, cols.stop - cols.start], F32, name=name)
-            nc.vector.tensor_copy(left[:], y[t][:].indirect(entries(lf_sb, cols)))
-            return left
+        def fetch_left(t, cols, into=None):
+            if into is None:
+                name = f"left{t}" if cols == wide else ["left_last0", "yy0_0"][t]
+                into = held.tile([P, cols.stop - cols.start], F32, name=name)[:]
+            nc.vector.tensor_copy(into, y[t][:].indirect(entries(lf_sb, cols)))
+            return into
 
         def times_right(prod, t, cols, left):
-            nc.vector.tensor_tensor(prod[:, t, : cols.stop - cols.start], gy[t][:].indirect(entries(rt_sb, cols)), left[:], MULT)
+            nc.vector.tensor_tensor(prod[:, t, : cols.stop - cols.start], gy[t][:].indirect(entries(rt_sb, cols)), left, MULT)
 
-        def subtract(prod, cols, at):
-            z_cols = z_grouped[:, cols.start * PACK : cols.stop * PACK].rearrange("p (c i t) -> p c t i", i=2, t=PACK)
-            nc.vector.tensor_tensor(z_cols, gyy[:, :, cols].rearrange("p t (c i) -> p c t i", i=2),
-                                    prod[:, :, at : at + cols.stop - cols.start].rearrange("p t (c i) -> p c t i", i=2), SUBTRACT)
+        def subtract(prod, cols, at, squares):
+            z_cols = z_grouped[cols.start][:].rearrange("p (c i t) -> p c t i", i=4, t=PACK)
+            nc.vector.tensor_tensor(z_cols, squares.rearrange("p t (c i) -> p c t i", i=4),
+                                    prod[:, :, at : at + cols.stop - cols.start].rearrange("p t (c i) -> p c t i", i=4), ADD)
 
         def score(cols, tags):
             width = cols.stop - cols.start
-            nc.vector.quantize_mx(z_words[:, cols].bitcast(FP8X4), z_scales[:, cols], z_grouped[:, cols.start * PACK : cols.stop * PACK])
+            nc.vector.quantize_mx(z_words[:, cols].bitcast(FP8X4), z_scales[:, cols], z_grouped[cols.start][:])
             per_bank = C // P // len(tags)
             banks = [psum.tile([P, per_bank, width], F32, name=tag) for tag in tags]
             for i in range(C // P):
@@ -164,7 +170,6 @@ def tile_picked_teager8_none_p_kernel(tc, x_words, x_scales, w1, gs, offs, lf, r
                     nc.scalar.activation(staged[:], bank[:], COPY, scale=0.0625)
                     (nc.scalar if on_vector else nc.sync).dma_start(rows, staged[:])
 
-        first, second = slice(0, 256), slice(256, WIDE)
         prod = held.tile([P, PACK, WIDE], F32, name="prod")
         left = fetch_left(0, wide)
         left_last = [fetch_left(0, last)]
@@ -172,17 +177,32 @@ def tile_picked_teager8_none_p_kernel(tc, x_words, x_scales, w1, gs, offs, lf, r
             ahead = fetch_left(t + 1, wide) if t + 1 < PACK else None
             times_right(prod, t, wide, left)
             left = ahead
+        turned = psum.tile([P, PACK, P], F32, name="y_bank0")
+        for t in range(PACK):
+            nc.tensor.matmul(turned[:, t, :], prod[:, t, second], identity[:], start=True, stop=False, is_transpose=True)
+            nc.tensor.matmul(turned[:, t, :], gyy[:, t, second], identity[:], start=False, stop=True, is_transpose=True)
+        z_rows = held.tile([P, H], BF16, name="z_rows")
+        nc.scalar.copy(z_rows[:].rearrange("j (u p e) -> j u p e", u=2, e=2), turned[:].rearrange("j (u e) p -> j u p e", u=2))
+        pairs = psum.tile([P, 2, P], F32, name="y_bank3")
+        for u in range(2):
+            nc.tensor.transpose(pairs[:, u, :], z_rows[:].bitcast(F32)[:, u * P : (u + 1) * P], identity[:])
+        nc.scalar.copy(z_grouped[second.start][:].bitcast(F32).rearrange("p (j u) -> p j u", u=2),
+                       pairs[:].rearrange("p u j -> p j u"))
+        gyy_last = held.tile([P, PACK, S - WIDE], F32, name="z_rows")
+        for t in range(PACK):
+            weighted_square(t, gyy_last, yy_last[t])
+
         left_last.append(fetch_left(1, last))
-        subtract(prod, first, 0)
-        left_last.append(fetch_left(2, last))
+        subtract(prod, first, 0, gyy[:, :, first])
+        late = held.tile([P, 2, S - WIDE], F32, name="yy3_0")
+        left_last.append(fetch_left(2, last, late[:, 0, :]))
         store(first, score(first, ["score_a", "score_b"]), [])
-        subtract(prod, second, 256)
         times_right(prod, 0, last, left_last[0])
-        left_last.append(fetch_left(3, last))
+        left_last.append(fetch_left(3, last, late[:, 1, :]))
         for t in range(1, PACK):
             times_right(prod, t, last, left_last[t])
         store(second, score(second, ["score_c"]), [])
-        subtract(prod, last, 0)
+        subtract(prod, last, 0, gyy_last[:])
         banks = score(last, ["score_d", "y_bank0", "y_bank1", "y_bank2"])
         by_scalar = held.tile([P, 2, S - WIDE], F32, name="by_scalar")
         by_vector = held.tile([P, 2, S - WIDE], F32, name="by_vector")

from contextlib import ExitStack

import concourse.mybir as mybir
from concourse.masks import make_identity

K, T, S, H, C = 512, 2048, 512, 512, 512
FLOPS = 2 * K * H * S + 2 * K * C * S

F32 = mybir.dt.float32
BF16 = mybir.dt.bfloat16
I32 = mybir.dt.int32
U32 = mybir.dt.uint32
U16 = mybir.dt.uint16
U8 = mybir.dt.uint8
FP8X4 = mybir.dt.float8_e4m3fn_x4
MULT = mybir.AluOpType.mult
ADD = mybir.AluOpType.add
COPY = mybir.ActivationFunctionType.Copy
SQUARE = mybir.ActivationFunctionType.Square

P = 128
PACK = 4
STRIPE = 16
WIDE = 384
W_CHUNKS = 2


def entries(offsets, cols):
    return offsets[:, cols.start // STRIPE : cols.stop // STRIPE]


def tile_picked_teager8_none_p_kernel(tc, x_words, x_scales, w1, gs, offs, lf, rt, cand, out):
    nc = tc.nc
    with ExitStack() as ctx:
        held = ctx.enter_context(tc.tile_pool(name="held", bufs=1))
        psum = ctx.enter_context(tc.psum_pool(name="psum", bufs=1))

        offs_sb = held.tile([P, S // STRIPE], U16, name="offs_sb")
        cand_sb = held.tile([P, C // STRIPE], U16, name="cand_sb")
        lf_sb = held.tile([P, S // STRIPE], U16, name="lf_sb")
        rt_sb = held.tile([P, S // STRIPE], U16, name="rt_sb")
        table_words = held.tile([P, T], U32, name="table_words", align_bytes=64)
        table_scales = held.tile([P, T], U8, name="table_scales", align_bytes=64)
        gain = held.tile([P, PACK], F32, name="gain")
        half_gain = held.tile([P, PACK], F32, name="half_gain")
        w_width = H // W_CHUNKS
        w_raw = [held.tile([P, PACK, w_width], F32, name=f"w_raw{c}") for c in range(W_CHUNKS)]

        nc.vector.memset(table_scales[:].bitcast(I32), 0)
        nc.sync.dma_start(offs_sb[:], offs)
        nc.sync.dma_start(cand_sb[:], cand)
        w_rows = w1.rearrange("(p j) h -> p j h", j=PACK)
        nc.sync.dma_start(w_raw[0][:], w_rows[:, :, :w_width])
        for r in range(4):
            nc.sync.dma_start(table_scales[r:P:32, :].bitcast(I32), x_scales[0, r:16:4, :].bitcast(I32))
        nc.sync.dma_start(w_raw[1][:], w_rows[:, :, w_width:])
        nc.sync.dma_start(table_words[:].bitcast(I32), x_words[0].rearrange("p n t -> p (n t)").bitcast(I32))
        nc.sync.dma_start(gain[:], gs.rearrange("(p t) o -> p (t o)", t=PACK))
        nc.sync.dma_start(lf_sb[:], lf)
        nc.sync.dma_start(rt_sb[:], rt)

        q_scales = held.tile([P, S], U8, name="q_scales", align_bytes=64)
        c_scales = held.tile([P, C], U8, name="c_scales", align_bytes=64)
        nc.vector.tensor_copy(q_scales[:], table_scales[:].indirect(offs_sb[:]))
        nc.vector.tensor_copy(c_scales[:], table_scales[:].indirect(cand_sb[:]))

        w_grouped = held.tile([P, H * PACK], BF16, name="w_grouped", align_bytes=64)
        w_dealt = w_grouped[:].rearrange("p (t m j) -> p m t j", t=PACK, j=PACK)
        m_width = w_width // PACK
        for c in range(W_CHUNKS):
            nc.scalar.activation(w_dealt[:, c * m_width : (c + 1) * m_width], w_raw[c][:].rearrange("p j (m t) -> p m t j", t=PACK), COPY)
        nc.scalar.activation(half_gain[:], gain[:], COPY, scale=0.5)
        minus_half_gain = held.tile([P, PACK], F32, name="minus_half_gain")
        nc.scalar.activation(minus_half_gain[:], gain[:], COPY, scale=-0.5)
        identity = held.tile([P, P], F32, name="identity")
        make_identity(nc, identity[:])
        w_words = held.tile([P, H], U32, name="w_words", align_bytes=64)
        w_scales = held.tile([P, H], U8, name="w_scales", align_bytes=64)
        for h in range(2):
            cols = slice(h * 256, (h + 1) * 256)
            nc.vector.quantize_mx(w_words[:, cols].bitcast(FP8X4), w_scales[:, cols], w_grouped[:, cols.start * PACK : cols.stop * PACK])

        halves = [slice(0, S // 2), slice(S // 2, S)]
        q_words = [held.tile([P, S // 2], U32, name=f"q_words{h}", align_bytes=64) for h in range(2)]
        for h, cols in enumerate(halves):
            nc.vector.tensor_copy(q_words[h][:], table_words[:].indirect(entries(offs_sb, cols)))
        c_words = held.tile([P, C], U32, name="c_words", align_bytes=64)
        nc.vector.tensor_copy(c_words[:], table_words[:].indirect(cand_sb[:]))

        y_bank = [psum.tile([P, S], F32, name=f"y_bank{t}") for t in range(PACK)]
        for t in range(PACK):
            rows = slice(t * P, (t + 1) * P)
            for h, cols in enumerate(halves):
                nc.tensor.matmul_mx(y_bank[t][:, cols], lhsT=w_words[:, rows].bitcast(FP8X4), lhsT_scale=w_scales[:, rows],
                                    rhs=q_words[h][:].bitcast(FP8X4), rhs_scale=q_scales[:, cols], start=True, stop=True)

        y = [held.tile([P, S], F32, name=f"y{t}") for t in range(PACK)]
        gy = [held.tile([P, S], F32, name=f"gy{t}") for t in range(PACK)]
        gyy = held.tile([P, PACK, WIDE], F32, name="gyy")

        def plain(t):
            nc.scalar.copy(y[t][:], y_bank[t][:])

        def weighted(t):
            nc.scalar.activation(gy[t][:], y_bank[t][:], COPY, scale=minus_half_gain[:, t : t + 1])

        def squared(t, cols):
            yy = held.tile([P, cols.stop - cols.start], F32, name=f"yy{t}_{cols.start}")
            nc.scalar.activation(yy[:], y[t][:, cols], SQUARE)
            return yy

        def weighted_square(t, into, yy):
            nc.scalar.activation(into[:, t, :], yy[:], COPY, scale=half_gain[:, t : t + 1])

        wide, last = slice(0, WIDE), slice(WIDE, S)
        plain(0)
        for t in range(PACK):
            if t + 1 < PACK:
                plain(t + 1)
            weighted(t)
        yy = squared(0, wide)
        for t in range(PACK):
            yy_ahead = squared(t + 1, wide) if t + 1 < PACK else None
            weighted_square(t, gyy, yy)
            yy = yy_ahead
        yy_last = [squared(t, last) for t in range(PACK)]

        z_words = held.tile([P, S], U32, name="z_words", align_bytes=64)
        z_scales = held.tile([P, S], U8, name="z_scales", align_bytes=64)
        first, second = slice(0, 256), slice(256, WIDE)
        z_grouped = {cols.start: held.tile([P, (cols.stop - cols.start) * PACK], BF16, name=f"z_grouped{cols.start}", align_bytes=64)
                     for cols in (first, second, last)}
        out_rows = out.rearrange("(i p) j -> p i j", p=P)

        def fetch_left(t, cols, into=None):
            if into is None:
                name = f"left{t}" if cols == wide else ["left_last0", "yy0_0"][t]
                into = held.tile([P, cols.stop - cols.start], F32, name=name)[:]
            nc.vector.tensor_copy(into, y[t][:].indirect(entries(lf_sb, cols)))
            return into

        def times_right(prod, t, cols, left):
            nc.vector.tensor_tensor(prod[:, t, : cols.stop - cols.start], gy[t][:].indirect(entries(rt_sb, cols)), left, MULT)

        def subtract(prod, cols, at, squares):
            z_cols = z_grouped[cols.start][:].rearrange("p (c i t) -> p c t i", i=4, t=PACK)
            nc.vector.tensor_tensor(z_cols, squares.rearrange("p t (c i) -> p c t i", i=4),
                                    prod[:, :, at : at + cols.stop - cols.start].rearrange("p t (c i) -> p c t i", i=4), ADD)

        def score(cols, tags):
            width = cols.stop - cols.start
            nc.vector.quantize_mx(z_words[:, cols].bitcast(FP8X4), z_scales[:, cols], z_grouped[cols.start][:])
            per_bank = C // P // len(tags)
            banks = [psum.tile([P, per_bank, width], F32, name=tag) for tag in tags]
            for i in range(C // P):
                rows = slice(i * P, (i + 1) * P)
                nc.tensor.matmul_mx(banks[i // per_bank][:, i % per_bank, :], lhsT=c_words[:, rows].bitcast(FP8X4), lhsT_scale=c_scales[:, rows],
                                    rhs=z_words[:, cols].bitcast(FP8X4), rhs_scale=z_scales[:, cols], start=True, stop=True)
            return banks

        def store(cols, banks, on_vector):
            per_bank = C // P // len(banks)
            for b, bank in enumerate(banks):
                staged = held.tile([P, per_bank, cols.stop - cols.start], F32, name=f"staged{cols.start}_{b}")
                rows = out_rows[:, b * per_bank : (b + 1) * per_bank, cols]
                if b in on_vector:
                    nc.vector.tensor_scalar_mul(staged[:], bank[:], 0.0625)
                    nc.sync.dma_start(rows, staged[:])
                else:
                    nc.scalar.activation(staged[:], bank[:], COPY, scale=0.0625)
                    (nc.scalar if on_vector else nc.sync).dma_start(rows, staged[:])

        prod = held.tile([P, PACK, WIDE], F32, name="prod")
        left = fetch_left(0, wide)
        left_last = [fetch_left(0, last)]
        for t in range(PACK):
            ahead = fetch_left(t + 1, wide) if t + 1 < PACK else None
            times_right(prod, t, wide, left)
            left = ahead
        turned = psum.tile([P, PACK, P], F32, name="y_bank0")
        for t in range(PACK):
            nc.tensor.matmul(turned[:, t, :], prod[:, t, second], identity[:], start=True, stop=False, is_transpose=True)
            nc.tensor.matmul(turned[:, t, :], gyy[:, t, second], identity[:], start=False, stop=True, is_transpose=True)
        z_rows = held.tile([P, H], BF16, name="z_rows")
        nc.scalar.copy(z_rows[:].rearrange("j (u p e) -> j u p e", u=2, e=2), turned[:].rearrange("j (u e) p -> j u p e", u=2))
        pairs = psum.tile([P, 2, P], F32, name="y_bank3")
        for u in range(2):
            nc.tensor.transpose(pairs[:, u, :], z_rows[:].bitcast(F32)[:, u * P : (u + 1) * P], identity[:])
        nc.scalar.copy(z_grouped[second.start][:].bitcast(F32).rearrange("p (j u) -> p j u", u=2),
                       pairs[:].rearrange("p u j -> p j u"))
        gyy_last = held.tile([P, PACK, S - WIDE], F32, name="z_rows")
        for t in range(PACK):
            weighted_square(t, gyy_last, yy_last[t])

        left_last.append(fetch_left(1, last))
        subtract(prod, first, 0, gyy[:, :, first])
        late = held.tile([P, 2, S - WIDE], F32, name="yy3_0")
        left_last.append(fetch_left(2, last, late[:, 0, :]))
        store(first, score(first, ["score_a", "score_b"]), [])
        times_right(prod, 0, last, left_last[0])
        left_last.append(fetch_left(3, last, late[:, 1, :]))
        for t in range(1, PACK):
            times_right(prod, t, last, left_last[t])
        store(second, score(second, ["score_c"]), [])
        subtract(prod, last, 0, gyy_last[:])
        banks = score(last, ["score_d", "y_bank0", "y_bank1", "y_bank2"])
        by_scalar = held.tile([P, 2, S - WIDE], F32, name="by_scalar")
        by_vector = held.tile([P, 2, S - WIDE], F32, name="by_vector")
        for n in range(2):
            nc.scalar.activation(by_scalar[:, n, :], banks[2 * n][:, 0, :], COPY, scale=0.0625)
            nc.vector.tensor_scalar_mul(by_vector[:, n, :], banks[2 * n + 1][:, 0, :], 0.0625)
        nc.scalar.dma_start(out_rows[:, 0::2, last], by_scalar[:])
        nc.sync.dma_start(out_rows[:, 1::2, last], by_vector[:])
